import numpy as np
import ml_dtypes


def mxq(x, axis, fmt="e4m3"):
    dtype, down = {"e4m3": (ml_dtypes.float8_e4m3fn, 7), "e5m2": (ml_dtypes.float8_e5m2, 14)}[fmt]
    v = np.moveaxis(np.asarray(x, np.float32).astype(ml_dtypes.bfloat16).astype(np.float64), axis, -1)
    blocks = v.reshape(v.shape[:-1] + (-1, 32))
    amax = np.abs(blocks).max(-1, keepdims=True)
    byte = np.maximum(np.where(amax > 0, np.frexp(amax)[1] - 1 + 127, 0) - down, 1)
    scale = np.exp2(byte - 127.0)
    codes = (blocks / scale).astype(np.float32).astype(dtype).astype(np.float64)
    return np.moveaxis((codes * scale).reshape(v.shape), -1, axis)


WIDE = False


def mx_kscale(k):
    if not WIDE:
        return np.ones(k)
    levels = np.array([10, -10, 5, -5, 0])
    if k % 512:
        return np.exp2(np.random.permutation(np.resize(levels, k // 32))).repeat(32)
    a = np.empty((k // 512, 16))
    for p in range(k // 512):
        a[p, :8] = np.random.permutation(np.resize(levels, 8))
        for g in range(8):
            far = levels[np.abs(levels - a[p, g]) >= 10]
            a[p, g + 8] = far[np.random.randint(len(far))]
    return np.exp2(a.ravel()).repeat(32)


def f64(x):
    return np.asarray(x).astype(np.float64)


def striped(idx):
    return np.tile(idx.reshape(-1, 16).T, (8, 1)).astype(np.uint16)


def unstriped(offs):
    return offs[:16].T.reshape(-1).astype(np.int64)


E2M1 = np.array([0.0, 0.5, 1.0, 1.5, 2.0, 3.0, 4.0, 6.0, -0.0, -0.5, -1.0, -1.5, -2.0, -3.0, -4.0, -6.0])


def pack_weight(w, fmt):
    k, n = w.shape
    w = f64(np.asarray(w, np.float32).astype(ml_dtypes.bfloat16)).reshape(k // 32, 32, n)
    amax = np.abs(w).max(1)
    if fmt == "e4m3":
        byte = np.frexp(amax)[1] - 1 + 127 - 7
    else:
        mant, ex = np.frexp(amax / 6.0)
        byte = np.where(mant > 0.5, ex, ex - 1) + 127
    byte = np.clip(np.where(amax > 0, byte, 1), 1, 254)
    scaled = (w * np.exp2(127.0 - byte)[:, None, :]).reshape(k, n).astype(np.float32)
    by_word = np.ascontiguousarray(scaled.reshape(k // 512, 128, 4, n).transpose(0, 1, 3, 2))
    if fmt == "e4m3":
        words = by_word.astype(ml_dtypes.float8_e4m3fn).view(np.uint8)
    else:
        c = by_word.astype(ml_dtypes.float4_e2m1fn).view(np.uint8) & 0xF
        words = (c[..., 0::2] | (c[..., 1::2] << 4)).reshape(k // 512, 128, 2 * n)
    return np.ascontiguousarray(words), np.ascontiguousarray(byte.astype(np.uint8).reshape(k // 512, 16, n))


def unpack_weight(words, scales, fmt):
    g, _, n = scales.shape
    words = np.ascontiguousarray(words).reshape(g, 128, n, -1)
    if fmt == "e4m3":
        vals = words.view(ml_dtypes.float8_e4m3fn).astype(np.float64)
    else:
        nib = np.empty((g, 128, n, 4), np.uint8)
        nib[..., 0::2] = words & 0xF
        nib[..., 1::2] = words >> 4
        vals = E2M1[nib]
    vals = vals * np.repeat(np.exp2(scales.astype(np.float64) - 127.0), 8, axis=1)[..., None]
    return vals.transpose(0, 1, 3, 2).reshape(g * 512, n)


def relu(v):
    return np.maximum(v, 0.0)


K, T, E, C, N = 1024, 640, 10, 128, 384


def by_expert(wq, xq):
    return np.concatenate([wq[e].T @ xq[:, e * C:(e + 1) * C] for e in range(E)], axis=1)


def setup_inputs():
    n = np.random.standard_normal
    s = mx_kscale(K)[:, None]
    first = np.random.permutation(np.repeat(np.arange(E), T // E))
    second = (first + 1 + np.random.permutation(np.repeat(np.arange(E - 1), -(-T // (E - 1)))[:T])) % E
    while np.bincount(second, minlength=E).max() != T // E:
        load = np.bincount(second, minlength=E); hi, lo = int(load.argmax()), int(load.argmin())
        t = np.flatnonzero((second == hi) & (first != lo))[0]; second[t] = lo
    slot_token = np.empty(E * C, np.int64); pos = np.empty((2, T), np.int64); fill = np.zeros(E, np.int64)
    place = np.stack([np.random.permutation(C) for _ in range(E)])
    for r, deal in enumerate((first, second)):
        for t in np.random.permutation(T):
            e = deal[t]; j = e * C + place[e, fill[e]]; fill[e] += 1; slot_token[j] = t; pos[r, t] = j
    g = np.random.uniform(0.2, 0.8, T)
    w = [pack_weight(m, "e2m1") for m in n((E, K, N)) / np.sqrt(K) / s[None]]
    w_slot = np.empty(E * C); w_slot[pos[0]] = g; w_slot[pos[1]] = 1.0 - g
    return {
        "xT": (n((K, T)) * s).astype(np.float32),
        "w_words": np.stack([m[0] for m in w]),
        "w_scales": np.stack([m[1] for m in w]),
        "b": (0.3 * n((N, E))).astype(np.float32),
        "gate": np.tile(w_slot, (K, 1)).astype(np.float32),
        "offs": striped(slot_token),
        "pos1": striped(pos[0]),
        "pos2": striped(pos[1]),
    }


def reference(xT, w_words, w_scales, b, gate, offs, pos1, pos2):
    idx = unstriped(offs)
    w = np.stack([unpack_weight(w_words[e], w_scales[e], "e2m1") for e in range(E)])
    xq = mxq(f64(gate) * f64(xT)[:, idx], 0, "e4m3")
    y = by_expert(w, xq)
    y = relu(y + np.repeat(f64(b), C, axis=1))
    return y[:, unstriped(pos1)] + y[:, unstriped(pos2)]

@@ -1,0 +1,160 @@
+from contextlib import ExitStack
+
+import concourse.mybir as mybir
+
+K, T, E, C, N = 1024, 640, 10, 128, 384
+S = E * C
+P = 128
+PACK = 4
+PASSES = K // (P * PACK)
+NB = N // P
+LIST = 16
+FLOPS = 2 * K * N * S
+BYTES = 4 * K * T + E * K * N // 2 + E * K * N // 32 + 4 * N * E + 4 * S + 2 * (S + 2 * T) + 4 * N * T
+
+F32 = mybir.dt.float32
+BF16 = mybir.dt.bfloat16
+I32 = mybir.dt.int32
+U32 = mybir.dt.uint32
+U16 = mybir.dt.uint16
+U8 = mybir.dt.uint8
+FP8X4 = mybir.dt.float8_e4m3fn_x4
+FP4X4 = mybir.dt.float4_e2m1fn_x4
+MULT = mybir.AluOpType.mult
+ADD = mybir.AluOpType.add
+COPY = mybir.ActivationFunctionType.Copy
+RELU = mybir.ActivationFunctionType.Relu
+
+CHUNK_EXPERTS = (4, 3, 2, 1)
+
+
+def tile_moe_pre_lin_relu_kernel(tc, xT, w_words, w_scales, b, gate, offs, pos1, pos2, out):
+    nc = tc.nc
+    firsts = [sum(CHUNK_EXPERTS[:c]) for c in range(len(CHUNK_EXPERTS))]
+
+    with ExitStack() as ctx:
+        keep = ctx.enter_context(tc.tile_pool(name="keep", bufs=1))
+        ring = ctx.enter_context(tc.tile_pool(name="ring", bufs=2))
+        psum = ctx.enter_context(tc.psum_pool(name="psum", bufs=2))
+
+        offs_sb = keep.tile([P, S // LIST], U16, name="offs_sb")
+        pos1_sb = keep.tile([P, T // LIST], U16, name="pos1_sb")
+        pos2_sb = keep.tile([P, T // LIST], U16, name="pos2_sb")
+        x_rows = xT.rearrange("(a p d) t -> a d p t", a=PASSES, d=PACK)
+        x_sb = {}
+        for a in range(PASSES):
+            for d in range(PACK):
+                x_sb[a, d] = keep.tile([P, T], F32, name="x_%d_%d" % (a, d))
+        gate_sb = [keep.tile([P, n * C], F32, name="gate_%d" % c) for c, n in enumerate(CHUNK_EXPERTS)]
+        w_sb = [keep.tile([P, n * PASSES, 2 * N], U8, name="w_%d" % c, align_bytes=64) for c, n in enumerate(CHUNK_EXPERTS)]
+        w_scale_sb = keep.tile([P, E * PASSES, N], U8, name="w_scale_sb", align_bytes=64)
+        b_sb = keep.tile([P, NB, E], F32, name="b_sb")
+        y_sb = [keep.tile([P, S], F32, name="y_%d" % j) for j in range(NB)]
+
+        def load_gate(c):
+            nc.sync.dma_start(gate_sb[c][:], gate[0:P, firsts[c] * C : (firsts[c] + CHUNK_EXPERTS[c]) * C])
+
+        def load_weights(c):
+            words = w_words[firsts[c] : firsts[c] + CHUNK_EXPERTS[c]].rearrange("e a p n -> p (e a) n")
+            nc.sync.dma_start(w_sb[c][:].bitcast(I32), words.bitcast(I32))
+
+        nc.vector.memset(w_scale_sb[:].bitcast(I32), 0)
+        nc.sync.dma_start(offs_sb[:], offs)
+        nc.sync.dma_start(x_sb[0, 0][:], x_rows[0, 0])
+        load_gate(0)
+        for a in range(PASSES):
+            for d in range(PACK):
+                if (a, d) != (0, 0):
+                    nc.sync.dma_start(x_sb[a, d][:], x_rows[a, d])
+        for c in range(1, len(CHUNK_EXPERTS)):
+            load_gate(c)
+        scale_rows = w_scales.rearrange("e a (q r) n -> r q (e a) n", r=4)
+        for r in range(4):
+            nc.sync.dma_start(w_scale_sb[r:P:32, :, :].bitcast(I32), scale_rows[r].bitcast(I32))
+        load_weights(0)
+        nc.sync.dma_start(b_sb[:], b.rearrange("(j p) e -> p j e", p=P))
+        for c in range(1, len(CHUNK_EXPERTS)):
+            load_weights(c)
+        nc.sync.dma_start(pos1_sb[:], pos1)
+        nc.sync.dma_start(pos2_sb[:], pos2)
+
+        steps = [(c, a) for c in range(len(CHUNK_EXPERTS)) for a in range(PASSES)]
+        gated = {}
+        codes = {}
+        scales = {}
+
+        def gather(step):
+            c, a = step
+            width = CHUNK_EXPERTS[c] * C
+            cols = slice(firsts[c] * C // LIST, (firsts[c] * C + width) // LIST)
+            gated[step] = ring.tile([P, PACK, width], F32, name="gated")
+            for d in range(PACK):
+                nc.vector.tensor_tensor(gated[step][:, d, :], x_sb[a, d][:].indirect(offs_sb[:, cols]), gate_sb[c][:], MULT)
+
+        def quantise(step):
+            c, a = step
+            width = CHUNK_EXPERTS[c] * C
+            woven = ring.tile([P, width * PACK], BF16, name="woven", align_bytes=64)
+            dst = woven[:].rearrange("p (g i d) -> p g d i", i=4, d=PACK)
+            src = gated[step][:].rearrange("p d (g i) -> p g d i", i=4)
+            if step == steps[-1]:
+                nc.vector.tensor_copy(dst, src)
+            else:
+                nc.scalar.activation(dst, src, COPY)
+            codes[step] = keep.tile([P, width], U32, name="codes_%d_%d" % step, align_bytes=64)
+            scales[step] = keep.tile([P, width], U8, name="scales_%d_%d" % step, align_bytes=64)
+            done = 0
+            for piece in (512, 256, 128):
+                if width - done >= piece:
+                    nc.vector.quantize_mx(
+                        out=codes[step][:, done : done + piece].bitcast(FP8X4),
+                        scales=scales[step][:, done : done + piece],
+                        in_=woven[:, done * PACK : (done + piece) * PACK],
+                    )
+                    done = done + piece
+
+        def experts(c):
+            for j in range(NB):
+                acc = psum.tile([P, 512], F32, name="acc_%d" % j)
+                for i in range(CHUNK_EXPERTS[c]):
+                    e = firsts[c] + i
+                    slots = slice(i * C, (i + 1) * C)
+                    for a in range(PASSES):
+                        nc.tensor.matmul_mx(
+                            out=acc[:, slots],
+                            lhsT=w_sb[c][:, i * PASSES + a, 2 * P * j : 2 * P * (j + 1)].bitcast(FP4X4),
+                            lhsT_scale=w_scale_sb[:, e * PASSES + a, P * j : P * (j + 1)],
+                            rhs=codes[c, a][:, slots].bitcast(FP8X4),
+                            rhs_scale=scales[c, a][:, slots],
+                            start=(a == 0),
+                            stop=(a == PASSES - 1),
+                        )
+                for i in range(CHUNK_EXPERTS[c]):
+                    e = firsts[c] + i
+                    nc.scalar.activation(
+                        y_sb[j][:, e * C : (e + 1) * C], acc[:, i * C : (i + 1) * C], RELU, bias=b_sb[:, j, e : e + 1]
+                    )
+
+        gather(steps[0])
+        for s, step in enumerate(steps):
+            if s + 1 < len(steps):
+                gather(steps[s + 1])
+            quantise(step)
+            if step[1] == PASSES - 1:
+                experts(step[0])
+
+        first = [keep.tile([P, T], F32, name="first_%d" % j) for j in range(NB)]
+        both = [keep.tile([P, T], F32, name="both_%d" % j) for j in range(NB)]
+
+        def fetch_first(j):
+            nc.vector.tensor_copy(first[j][:], y_sb[j][:].indirect(pos1_sb[:]))
+
+        def add_second(j):
+            nc.vector.tensor_tensor(both[j][:], y_sb[j][:].indirect(pos2_sb[:]), first[j][:], ADD)
+            nc.sync.dma_start(out[j * P : (j + 1) * P, :], both[j][:])
+
+        fetch_first(0)
+        for j in range(NB):
+            if j + 1 < NB:
+                fetch_first(j + 1)
+            add_second(j)

@@ -22,20 +22,26 @@ FP8X4 = mybir.dt.float8_e4m3fn_x4
 FP4X4 = mybir.dt.float4_e2m1fn_x4
 MULT = mybir.AluOpType.mult
 ADD = mybir.AluOpType.add
+MAX = mybir.AluOpType.max
 COPY = mybir.ActivationFunctionType.Copy
 RELU = mybir.ActivationFunctionType.Relu
 
-CHUNK_EXPERTS = (4, 3, 2, 1)
+STEPS = ((0, 0, 4), (1, 0, 4), (0, 4, 6), (1, 4, 3), (1, 7, 2), (1, 9, 1))
+GATE_CUTS = (0, 128, 512, 1280)
+HEAD = 128
+TAIL = 128
 
 
 def tile_moe_pre_lin_relu_kernel(tc, xT, w_words, w_scales, b, gate, offs, pos1, pos2, out):
     nc = tc.nc
-    firsts = [sum(CHUNK_EXPERTS[:c]) for c in range(len(CHUNK_EXPERTS))]
+    groups = [(e0, n) for a, e0, n in STEPS if a == PASSES - 1]
+    widest = [max(n for a2, e0, n in STEPS if a2 == a) * C for a in range(PASSES)]
+    window = [T if widest[a] < T else widest[a] + LIST for a in range(PASSES)]
 
     with ExitStack() as ctx:
         keep = ctx.enter_context(tc.tile_pool(name="keep", bufs=1))
         ring = ctx.enter_context(tc.tile_pool(name="ring", bufs=2))
-        psum = ctx.enter_context(tc.psum_pool(name="psum", bufs=2))
+        psum = ctx.enter_context(tc.psum_pool(name="psum", bufs=1))
 
         offs_sb = keep.tile([P, S // LIST], U16, name="offs_sb")
         pos1_sb = keep.tile([P, T // LIST], U16, name="pos1_sb")
@@ -44,104 +50,135 @@ def tile_moe_pre_lin_relu_kernel(tc, xT, w_words, w_scales, b, gate, offs, pos1,
         x_sb = {}
         for a in range(PASSES):
             for d in range(PACK):
-                x_sb[a, d] = keep.tile([P, T], F32, name="x_%d_%d" % (a, d))
-        gate_sb = [keep.tile([P, n * C], F32, name="gate_%d" % c) for c, n in enumerate(CHUNK_EXPERTS)]
-        w_sb = [keep.tile([P, n * PASSES, 2 * N], U8, name="w_%d" % c, align_bytes=64) for c, n in enumerate(CHUNK_EXPERTS)]
+                x_sb[a, d] = keep.tile([P, window[a]], F32, name="x_%d_%d" % (a, d))
+        gate_sb = keep.tile([P, S], F32, name="gate_sb")
+        w_sb = [keep.tile([P, n * PASSES, 2 * N], U8, name="w_%d" % e0, align_bytes=64) for e0, n in groups]
         w_scale_sb = keep.tile([P, E * PASSES, N], U8, name="w_scale_sb", align_bytes=64)
         b_sb = keep.tile([P, NB, E], F32, name="b_sb")
         y_sb = [keep.tile([P, S], F32, name="y_%d" % j) for j in range(NB)]
+        codes = [keep.tile([P, S], U32, name="codes_%d" % a, align_bytes=64) for a in range(PASSES)]
+        scales = [keep.tile([P, S], U8, name="scales_%d" % a, align_bytes=64) for a in range(PASSES)]
 
         def load_gate(c):
-            nc.sync.dma_start(gate_sb[c][:], gate[0:P, firsts[c] * C : (firsts[c] + CHUNK_EXPERTS[c]) * C])
+            nc.sync.dma_start(gate_sb[:, GATE_CUTS[c] : GATE_CUTS[c + 1]], gate[0:P, GATE_CUTS[c] : GATE_CUTS[c + 1]])
 
-        def load_weights(c):
-            words = w_words[firsts[c] : firsts[c] + CHUNK_EXPERTS[c]].rearrange("e a p n -> p (e a) n")
-            nc.sync.dma_start(w_sb[c][:].bitcast(I32), words.bitcast(I32))
+        def load_x(a, d):
+            nc.sync.dma_start(x_sb[a, d][:, 0:T], x_rows[a, d])
 
+        def load_weights(g):
+            e0, n = groups[g]
+            words = w_words[e0 : e0 + n].rearrange("e a p n -> p (e a) n")
+            nc.sync.dma_start(w_sb[g][:].bitcast(I32), words.bitcast(I32))
+
+        for a in range(PASSES):
+            for d in range(PACK):
+                if window[a] > T:
+                    nc.vector.memset(x_sb[a, d][:, T:], 0.0)
         nc.vector.memset(w_scale_sb[:].bitcast(I32), 0)
+        load_x(0, 0)
         nc.sync.dma_start(offs_sb[:], offs)
-        nc.sync.dma_start(x_sb[0, 0][:], x_rows[0, 0])
-        load_gate(0)
+        for c in range(len(GATE_CUTS) - 2):
+            load_gate(c)
         for a in range(PASSES):
             for d in range(PACK):
                 if (a, d) != (0, 0):
-                    nc.sync.dma_start(x_sb[a, d][:], x_rows[a, d])
-        for c in range(1, len(CHUNK_EXPERTS)):
-            load_gate(c)
+                    load_x(a, d)
+        load_gate(len(GATE_CUTS) - 2)
         scale_rows = w_scales.rearrange("e a (q r) n -> r q (e a) n", r=4)
         for r in range(4):
             nc.sync.dma_start(w_scale_sb[r:P:32, :, :].bitcast(I32), scale_rows[r].bitcast(I32))
         load_weights(0)
         nc.sync.dma_start(b_sb[:], b.rearrange("(j p) e -> p j e", p=P))
-        for c in range(1, len(CHUNK_EXPERTS)):
-            load_weights(c)
+        for g in range(1, len(groups)):
+            load_weights(g)
         nc.sync.dma_start(pos1_sb[:], pos1)
         nc.sync.dma_start(pos2_sb[:], pos2)
 
-        steps = [(c, a) for c in range(len(CHUNK_EXPERTS)) for a in range(PASSES)]
         gated = {}
-        codes = {}
-        scales = {}
 
         def gather(step):
-            c, a = step
-            width = CHUNK_EXPERTS[c] * C
-            cols = slice(firsts[c] * C // LIST, (firsts[c] * C + width) // LIST)
-            gated[step] = ring.tile([P, PACK, width], F32, name="gated")
+            a, e0, n = step
+            gated[step] = ring.tile([P, PACK, n * C], F32, name="gated")
             for d in range(PACK):
-                nc.vector.tensor_tensor(gated[step][:, d, :], x_sb[a, d][:].indirect(offs_sb[:, cols]), gate_sb[c][:], MULT)
+                cuts = [0, HEAD, n * C] if (step == STEPS[0] and d == 0 and HEAD) else [0, n * C]
+                for lo, hi in zip(cuts, cuts[1:]):
+                    nc.vector.tensor_tensor(
+                        gated[step][:, d, lo:hi],
+                        x_sb[a, d][:].indirect(offs_sb[:, (e0 * C + lo) // LIST : (e0 * C + hi) // LIST]),
+                        gate_sb[:, e0 * C + lo : e0 * C + hi],
+                        MULT,
+                    )
 
-        def quantise(step):
-            c, a = step
-            width = CHUNK_EXPERTS[c] * C
-            woven = ring.tile([P, width * PACK], BF16, name="woven", align_bytes=64)
-            dst = woven[:].rearrange("p (g i d) -> p g d i", i=4, d=PACK)
+        woven = {}
+
+        def weave(step):
+            woven[step] = ring.tile([P, step[2] * C * PACK], BF16, name="woven", align_bytes=64)
+            dst = woven[step][:].rearrange("p (g i d) -> p g d i", i=4, d=PACK)
             src = gated[step][:].rearrange("p d (g i) -> p g d i", i=4)
-            if step == steps[-1]:
+            if step == STEPS[-1]:
                 nc.vector.tensor_copy(dst, src)
             else:
                 nc.scalar.activation(dst, src, COPY)
-            codes[step] = keep.tile([P, width], U32, name="codes_%d_%d" % step, align_bytes=64)
-            scales[step] = keep.tile([P, width], U8, name="scales_%d_%d" % step, align_bytes=64)
-            done = 0
+
+        def quantise(step, lo, hi):
+            a, e0, n = step
             for piece in (512, 256, 128):
-                if width - done >= piece:
+                if hi - lo >= piece:
+                    cols = slice(e0 * C + lo, e0 * C + lo + piece)
                     nc.vector.quantize_mx(
-                        out=codes[step][:, done : done + piece].bitcast(FP8X4),
-                        scales=scales[step][:, done : done + piece],
-                        in_=woven[:, done * PACK : (done + piece) * PACK],
+                        out=codes[a][:, cols].bitcast(FP8X4),
+                        scales=scales[a][:, cols],
+                        in_=woven[step][:, lo * PACK : (lo + piece) * PACK],
                     )
-                    done = done + piece
+                    lo = lo + piece
 
-        def experts(c):
-            for j in range(NB):
-                acc = psum.tile([P, 512], F32, name="acc_%d" % j)
-                for i in range(CHUNK_EXPERTS[c]):
-                    e = firsts[c] + i
-                    slots = slice(i * C, (i + 1) * C)
-                    for a in range(PASSES):
-                        nc.tensor.matmul_mx(
-                            out=acc[:, slots],
-                            lhsT=w_sb[c][:, i * PASSES + a, 2 * P * j : 2 * P * (j + 1)].bitcast(FP4X4),
-                            lhsT_scale=w_scale_sb[:, e * PASSES + a, P * j : P * (j + 1)],
-                            rhs=codes[c, a][:, slots].bitcast(FP8X4),
-                            rhs_scale=scales[c, a][:, slots],
-                            start=(a == 0),
-                            stop=(a == PASSES - 1),
-                        )
-                for i in range(CHUNK_EXPERTS[c]):
-                    e = firsts[c] + i
-                    nc.scalar.activation(
-                        y_sb[j][:, e * C : (e + 1) * C], acc[:, i * C : (i + 1) * C], RELU, bias=b_sb[:, j, e : e + 1]
+        banks = [psum.tile([P, 512], F32, name="bank_%d" % i) for i in range(8)]
+        home = {e: (g, e - e0) for g, (e0, n) in enumerate(groups) for e in range(e0, e0 + n)}
+
+        def products(j, experts, bank, on_vector=False):
+            acc = banks[bank]
+            for i, e in enumerate(experts):
+                g, place = home[e]
+                slots = slice(e * C, (e + 1) * C)
+                for a in range(PASSES):
+                    nc.tensor.matmul_mx(
+                        out=acc[:, i * C : (i + 1) * C],
+                        lhsT=w_sb[g][:, place * PASSES + a, 2 * P * j : 2 * P * (j + 1)].bitcast(FP4X4),
+                        lhsT_scale=w_scale_sb[:, e * PASSES + a, P * j : P * (j + 1)],
+                        rhs=codes[a][:, slots].bitcast(FP8X4),
+                        rhs_scale=scales[a][:, slots],
+                        start=(a == 0),
+                        stop=(a == PASSES - 1),
                     )
+            for i, e in enumerate(experts):
+                dst, src, bias = y_sb[j][:, e * C : (e + 1) * C], acc[:, i * C : (i + 1) * C], b_sb[:, j, e : e + 1]
+                if on_vector:
+                    nc.vector.tensor_scalar(dst, src, bias, 0.0, ADD, MAX)
+                else:
+                    nc.scalar.activation(dst, src, RELU, bias=bias)
 
-        gather(steps[0])
-        for s, step in enumerate(steps):
-            if s + 1 < len(steps):
-                gather(steps[s + 1])
-            quantise(step)
-            if step[1] == PASSES - 1:
-                experts(step[0])
+        gather(STEPS[0])
+        for s in range(4):
+            gather(STEPS[s + 1])
+            weave(STEPS[s])
+            quantise(STEPS[s], 0, STEPS[s][2] * C)
+            if s == 1:
+                for j in range(NB):
+                    products(j, range(0, 4), j)
+        weave(STEPS[4])
+        products(0, range(4, 7), 3)
+        products(1, range(4, 7), 4)
+        gather(STEPS[5])
+        quantise(STEPS[4], 0, C)
+        weave(STEPS[5])
+        quantise(STEPS[4], C, 2 * C)
+        quantise(STEPS[5], 0, C)
+        products(0, range(7, 9), 5)
+        products(0, range(9, 10), 6, True)
+        products(1, range(7, 9), 0)
+        products(1, range(9, 10), 7)
+        products(2, range(4, 7), 6)
+        products(2, range(7, 10), 7)
 
         first = [keep.tile([P, T], F32, name="first_%d" % j) for j in range(NB)]
         both = [keep.tile([P, T], F32, name="both_%d" % j) for j in range(NB)]
@@ -149,12 +186,17 @@ def tile_moe_pre_lin_relu_kernel(tc, xT, w_words, w_scales, b, gate, offs, pos1,
         def fetch_first(j):
             nc.vector.tensor_copy(first[j][:], y_sb[j][:].indirect(pos1_sb[:]))
 
-        def add_second(j):
-            nc.vector.tensor_tensor(both[j][:], y_sb[j][:].indirect(pos2_sb[:]), first[j][:], ADD)
-            nc.sync.dma_start(out[j * P : (j + 1) * P, :], both[j][:])
+        def add_second(j, lo, hi):
+            nc.vector.tensor_tensor(
+                both[j][:, lo:hi], y_sb[j][:].indirect(pos2_sb[:, lo // LIST : hi // LIST]), first[j][:, lo:hi], ADD
+            )
+            nc.sync.dma_start(out[j * P : (j + 1) * P, lo:hi], both[j][:, lo:hi])
 
         fetch_first(0)
         for j in range(NB):
             if j + 1 < NB:
                 fetch_first(j + 1)
-            add_second(j)
+                add_second(j, 0, T)
+            else:
+                add_second(j, 0, T - TAIL)
+                add_second(j, T - TAIL, T)

@@ -29,7 +29,7 @@ RELU = mybir.ActivationFunctionType.Relu
 STEPS = ((0, 0, 4), (1, 0, 4), (0, 4, 6), (1, 4, 3), (1, 7, 2), (1, 9, 1))
 GATE_CUTS = (0, 128, 512, 1280)
 HEAD = 128
-TAIL = 128
+TAIL = (0, 352, 512, 640)
 
 
 def tile_moe_pre_lin_relu_kernel(tc, xT, w_words, w_scales, b, gate, offs, pos1, pos2, out):
@@ -60,7 +60,7 @@ def tile_moe_pre_lin_relu_kernel(tc, xT, w_words, w_scales, b, gate, offs, pos1,
         scales = [keep.tile([P, S], U8, name="scales_%d" % a, align_bytes=64) for a in range(PASSES)]
 
         def load_gate(c):
-            nc.sync.dma_start(gate_sb[:, GATE_CUTS[c] : GATE_CUTS[c + 1]], gate[0:P, GATE_CUTS[c] : GATE_CUTS[c + 1]])
+            (nc.scalar if c == 0 else nc.sync).dma_start(gate_sb[:, GATE_CUTS[c] : GATE_CUTS[c + 1]], gate[0:P, GATE_CUTS[c] : GATE_CUTS[c + 1]])
 
         def load_x(a, d):
             nc.sync.dma_start(x_sb[a, d][:, 0:T], x_rows[a, d])
@@ -173,7 +173,7 @@ def tile_moe_pre_lin_relu_kernel(tc, xT, w_words, w_scales, b, gate, offs, pos1,
         weave(STEPS[5])
         quantise(STEPS[4], C, 2 * C)
         quantise(STEPS[5], 0, C)
-        products(0, range(7, 9), 5)
+        products(0, range(7, 9), 5, True)
         products(0, range(9, 10), 6, True)
         products(1, range(7, 9), 0)
         products(1, range(9, 10), 7)
@@ -198,5 +198,5 @@ def tile_moe_pre_lin_relu_kernel(tc, xT, w_words, w_scales, b, gate, offs, pos1,
                 fetch_first(j + 1)
                 add_second(j, 0, T)
             else:
-                add_second(j, 0, T - TAIL)
-                add_second(j, T - TAIL, T)
+                for lo, hi in zip(TAIL, TAIL[1:]):
+                    add_second(j, lo, hi)

from contextlib import ExitStack

import concourse.mybir as mybir

K, T, E, C, N = 1024, 640, 10, 128, 384
S = E * C
P = 128
PACK = 4
PASSES = K // (P * PACK)
NB = N // P
LIST = 16
FLOPS = 2 * K * N * S
BYTES = 4 * K * T + E * K * N // 2 + E * K * N // 32 + 4 * N * E + 4 * S + 2 * (S + 2 * T) + 4 * N * T

F32 = mybir.dt.float32
BF16 = mybir.dt.bfloat16
I32 = mybir.dt.int32
U32 = mybir.dt.uint32
U16 = mybir.dt.uint16
U8 = mybir.dt.uint8
FP8X4 = mybir.dt.float8_e4m3fn_x4
FP4X4 = mybir.dt.float4_e2m1fn_x4
MULT = mybir.AluOpType.mult
ADD = mybir.AluOpType.add
MAX = mybir.AluOpType.max
COPY = mybir.ActivationFunctionType.Copy
RELU = mybir.ActivationFunctionType.Relu

STEPS = ((0, 0, 4), (1, 0, 4), (0, 4, 6), (1, 4, 3), (1, 7, 2), (1, 9, 1))
GATE_CUTS = (0, 128, 512, 1280)
HEAD = 128
TAIL = (0, 352, 512, 640)


def tile_moe_pre_lin_relu_kernel(tc, xT, w_words, w_scales, b, gate, offs, pos1, pos2, out):
    nc = tc.nc
    groups = [(e0, n) for a, e0, n in STEPS if a == PASSES - 1]
    widest = [max(n for a2, e0, n in STEPS if a2 == a) * C for a in range(PASSES)]
    window = [T if widest[a] < T else widest[a] + LIST for a in range(PASSES)]

    with ExitStack() as ctx:
        keep = ctx.enter_context(tc.tile_pool(name="keep", bufs=1))
        ring = ctx.enter_context(tc.tile_pool(name="ring", bufs=2))
        psum = ctx.enter_context(tc.psum_pool(name="psum", bufs=1))

        offs_sb = keep.tile([P, S // LIST], U16, name="offs_sb")
        pos1_sb = keep.tile([P, T // LIST], U16, name="pos1_sb")
        pos2_sb = keep.tile([P, T // LIST], U16, name="pos2_sb")
        x_rows = xT.rearrange("(a p d) t -> a d p t", a=PASSES, d=PACK)
        x_sb = {}
        for a in range(PASSES):
            for d in range(PACK):
                x_sb[a, d] = keep.tile([P, window[a]], F32, name="x_%d_%d" % (a, d))
        gate_sb = keep.tile([P, S], F32, name="gate_sb")
        w_sb = [keep.tile([P, n * PASSES, 2 * N], U8, name="w_%d" % e0, align_bytes=64) for e0, n in groups]
        w_scale_sb = keep.tile([P, E * PASSES, N], U8, name="w_scale_sb", align_bytes=64)
        b_sb = keep.tile([P, NB, E], F32, name="b_sb")
        y_sb = [keep.tile([P, S], F32, name="y_%d" % j) for j in range(NB)]
        codes = [keep.tile([P, S], U32, name="codes_%d" % a, align_bytes=64) for a in range(PASSES)]
        scales = [keep.tile([P, S], U8, name="scales_%d" % a, align_bytes=64) for a in range(PASSES)]

        def load_gate(c):
            (nc.scalar if c == 0 else nc.sync).dma_start(gate_sb[:, GATE_CUTS[c] : GATE_CUTS[c + 1]], gate[0:P, GATE_CUTS[c] : GATE_CUTS[c + 1]])

        def load_x(a, d):
            nc.sync.dma_start(x_sb[a, d][:, 0:T], x_rows[a, d])

        def load_weights(g):
            e0, n = groups[g]
            words = w_words[e0 : e0 + n].rearrange("e a p n -> p (e a) n")
            nc.sync.dma_start(w_sb[g][:].bitcast(I32), words.bitcast(I32))

        for a in range(PASSES):
            for d in range(PACK):
                if window[a] > T:
                    nc.vector.memset(x_sb[a, d][:, T:], 0.0)
        nc.vector.memset(w_scale_sb[:].bitcast(I32), 0)
        load_x(0, 0)
        nc.sync.dma_start(offs_sb[:], offs)
        for c in range(len(GATE_CUTS) - 2):
            load_gate(c)
        for a in range(PASSES):
            for d in range(PACK):
                if (a, d) != (0, 0):
                    load_x(a, d)
        load_gate(len(GATE_CUTS) - 2)
        scale_rows = w_scales.rearrange("e a (q r) n -> r q (e a) n", r=4)
        for r in range(4):
            nc.sync.dma_start(w_scale_sb[r:P:32, :, :].bitcast(I32), scale_rows[r].bitcast(I32))
        load_weights(0)
        nc.sync.dma_start(b_sb[:], b.rearrange("(j p) e -> p j e", p=P))
        for g in range(1, len(groups)):
            load_weights(g)
        nc.sync.dma_start(pos1_sb[:], pos1)
        nc.sync.dma_start(pos2_sb[:], pos2)

        gated = {}

        def gather(step):
            a, e0, n = step
            gated[step] = ring.tile([P, PACK, n * C], F32, name="gated")
            for d in range(PACK):
                cuts = [0, HEAD, n * C] if (step == STEPS[0] and d == 0 and HEAD) else [0, n * C]
                for lo, hi in zip(cuts, cuts[1:]):
                    nc.vector.tensor_tensor(
                        gated[step][:, d, lo:hi],
                        x_sb[a, d][:].indirect(offs_sb[:, (e0 * C + lo) // LIST : (e0 * C + hi) // LIST]),
                        gate_sb[:, e0 * C + lo : e0 * C + hi],
                        MULT,
                    )

        woven = {}

        def weave(step):
            woven[step] = ring.tile([P, step[2] * C * PACK], BF16, name="woven", align_bytes=64)
            dst = woven[step][:].rearrange("p (g i d) -> p g d i", i=4, d=PACK)
            src = gated[step][:].rearrange("p d (g i) -> p g d i", i=4)
            if step == STEPS[-1]:
                nc.vector.tensor_copy(dst, src)
            else:
                nc.scalar.activation(dst, src, COPY)

        def quantise(step, lo, hi):
            a, e0, n = step
            for piece in (512, 256, 128):
                if hi - lo >= piece:
                    cols = slice(e0 * C + lo, e0 * C + lo + piece)
                    nc.vector.quantize_mx(
                        out=codes[a][:, cols].bitcast(FP8X4),
                        scales=scales[a][:, cols],
                        in_=woven[step][:, lo * PACK : (lo + piece) * PACK],
                    )
                    lo = lo + piece

        banks = [psum.tile([P, 512], F32, name="bank_%d" % i) for i in range(8)]
        home = {e: (g, e - e0) for g, (e0, n) in enumerate(groups) for e in range(e0, e0 + n)}

        def products(j, experts, bank, on_vector=False):
            acc = banks[bank]
            for i, e in enumerate(experts):
                g, place = home[e]
                slots = slice(e * C, (e + 1) * C)
                for a in range(PASSES):
                    nc.tensor.matmul_mx(
                        out=acc[:, i * C : (i + 1) * C],
                        lhsT=w_sb[g][:, place * PASSES + a, 2 * P * j : 2 * P * (j + 1)].bitcast(FP4X4),
                        lhsT_scale=w_scale_sb[:, e * PASSES + a, P * j : P * (j + 1)],
                        rhs=codes[a][:, slots].bitcast(FP8X4),
                        rhs_scale=scales[a][:, slots],
                        start=(a == 0),
                        stop=(a == PASSES - 1),
                    )
            for i, e in enumerate(experts):
                dst, src, bias = y_sb[j][:, e * C : (e + 1) * C], acc[:, i * C : (i + 1) * C], b_sb[:, j, e : e + 1]
                if on_vector:
                    nc.vector.tensor_scalar(dst, src, bias, 0.0, ADD, MAX)
                else:
                    nc.scalar.activation(dst, src, RELU, bias=bias)

        gather(STEPS[0])
        for s in range(4):
            gather(STEPS[s + 1])
            weave(STEPS[s])
            quantise(STEPS[s], 0, STEPS[s][2] * C)
            if s == 1:
                for j in range(NB):
                    products(j, range(0, 4), j)
        weave(STEPS[4])
        products(0, range(4, 7), 3)
        products(1, range(4, 7), 4)
        gather(STEPS[5])
        quantise(STEPS[4], 0, C)
        weave(STEPS[5])
        quantise(STEPS[4], C, 2 * C)
        quantise(STEPS[5], 0, C)
        products(0, range(7, 9), 5, True)
        products(0, range(9, 10), 6, True)
        products(1, range(7, 9), 0)
        products(1, range(9, 10), 7)
        products(2, range(4, 7), 6)
        products(2, range(7, 10), 7)

        first = [keep.tile([P, T], F32, name="first_%d" % j) for j in range(NB)]
        both = [keep.tile([P, T], F32, name="both_%d" % j) for j in range(NB)]

        def fetch_first(j):
            nc.vector.tensor_copy(first[j][:], y_sb[j][:].indirect(pos1_sb[:]))

        def add_second(j, lo, hi):
            nc.vector.tensor_tensor(
                both[j][:, lo:hi], y_sb[j][:].indirect(pos2_sb[:, lo // LIST : hi // LIST]), first[j][:, lo:hi], ADD
            )
            nc.sync.dma_start(out[j * P : (j + 1) * P, lo:hi], both[j][:, lo:hi])

        fetch_first(0)
        for j in range(NB):
            if j + 1 < NB:
                fetch_first(j + 1)
                add_second(j, 0, T)
            else:
                for lo, hi in zip(TAIL, TAIL[1:]):
                    add_second(j, lo, hi)
